import numpy as np
import ml_dtypes


def mxq(x, axis, fmt="e4m3"):
    dtype, down = {"e4m3": (ml_dtypes.float8_e4m3fn, 7), "e5m2": (ml_dtypes.float8_e5m2, 14)}[fmt]
    v = np.moveaxis(np.asarray(x, np.float32).astype(ml_dtypes.bfloat16).astype(np.float64), axis, -1)
    blocks = v.reshape(v.shape[:-1] + (-1, 32))
    amax = np.abs(blocks).max(-1, keepdims=True)
    byte = np.maximum(np.where(amax > 0, np.frexp(amax)[1] - 1 + 127, 0) - down, 1)
    scale = np.exp2(byte - 127.0)
    codes = (blocks / scale).astype(np.float32).astype(dtype).astype(np.float64)
    return np.moveaxis((codes * scale).reshape(v.shape), -1, axis)


WIDE = False


def mx_kscale(k):
    if not WIDE:
        return np.ones(k)
    levels = np.array([10, -10, 5, -5, 0])
    if k % 512:
        return np.exp2(np.random.permutation(np.resize(levels, k // 32))).repeat(32)
    a = np.empty((k // 512, 16))
    for p in range(k // 512):
        a[p, :8] = np.random.permutation(np.resize(levels, 8))
        for g in range(8):
            far = levels[np.abs(levels - a[p, g]) >= 10]
            a[p, g + 8] = far[np.random.randint(len(far))]
    return np.exp2(a.ravel()).repeat(32)


def f64(x):
    return np.asarray(x).astype(np.float64)


def striped(idx):
    return np.tile(idx.reshape(-1, 16).T, (8, 1)).astype(np.uint16)


def unstriped(offs):
    return offs[:16].T.reshape(-1).astype(np.int64)


E2M1 = np.array([0.0, 0.5, 1.0, 1.5, 2.0, 3.0, 4.0, 6.0, -0.0, -0.5, -1.0, -1.5, -2.0, -3.0, -4.0, -6.0])


def pack_weight(w, fmt):
    k, n = w.shape
    w = f64(np.asarray(w, np.float32).astype(ml_dtypes.bfloat16)).reshape(k // 32, 32, n)
    amax = np.abs(w).max(1)
    if fmt == "e4m3":
        byte = np.frexp(amax)[1] - 1 + 127 - 7
    else:
        mant, ex = np.frexp(amax / 6.0)
        byte = np.where(mant > 0.5, ex, ex - 1) + 127
    byte = np.clip(np.where(amax > 0, byte, 1), 1, 254)
    scaled = (w * np.exp2(127.0 - byte)[:, None, :]).reshape(k, n).astype(np.float32)
    by_word = np.ascontiguousarray(scaled.reshape(k // 512, 128, 4, n).transpose(0, 1, 3, 2))
    if fmt == "e4m3":
        words = by_word.astype(ml_dtypes.float8_e4m3fn).view(np.uint8)
    else:
        c = by_word.astype(ml_dtypes.float4_e2m1fn).view(np.uint8) & 0xF
        words = (c[..., 0::2] | (c[..., 1::2] << 4)).reshape(k // 512, 128, 2 * n)
    return np.ascontiguousarray(words), np.ascontiguousarray(byte.astype(np.uint8).reshape(k // 512, 16, n))


def unpack_weight(words, scales, fmt):
    g, _, n = scales.shape
    words = np.ascontiguousarray(words).reshape(g, 128, n, -1)
    if fmt == "e4m3":
        vals = words.view(ml_dtypes.float8_e4m3fn).astype(np.float64)
    else:
        nib = np.empty((g, 128, n, 4), np.uint8)
        nib[..., 0::2] = words & 0xF
        nib[..., 1::2] = words >> 4
        vals = E2M1[nib]
    vals = vals * np.repeat(np.exp2(scales.astype(np.float64) - 127.0), 8, axis=1)[..., None]
    return vals.transpose(0, 1, 3, 2).reshape(g * 512, n)


def gelu(v):
    return 0.5 * v * (1.0 + np.tanh(np.sqrt(2.0 / np.pi) * (v + 0.044715 * v**3)))


def bf(x):
    return np.asarray(x, np.float32).astype(ml_dtypes.bfloat16)

def planes(Y):
    n, m = Y.shape
    b = f64(bf(Y)).reshape(n // 32, 32, m)
    amax = np.abs(b).max(1)
    byte = np.clip(np.where(amax > 0, np.frexp(amax)[1] - 1 + 127 - 7, 1), 1, 254)
    codes = (b * np.exp2(127.0 - byte)[:, None, :]).reshape(n, m).astype(np.float32).astype(ml_dtypes.float8_e4m3fn).view(np.uint8)
    words = codes.reshape(n // 512, 128, 4, m).transpose(0, 1, 3, 2)
    return np.ascontiguousarray(words), np.ascontiguousarray(byte.astype(np.uint8).reshape(n // 512, 16, m))


K, H, N, T, S = 1024, 512, 1024, 2048, 1024

def setup_inputs():
    n = np.random.standard_normal
    s = mx_kscale(K)[:, None]
    u = mx_kscale(H)[:, None]
    tab_words, tab_scales = pack_weight(n((K, T)) * s, "e4m3")
    w1 = 0.5 * n((K, H)) / np.sqrt(K) / s
    w2_words, w2_scales = pack_weight(0.5 * n((K, H)) / np.sqrt(K) / s, "e2m1")
    w3_words, w3_scales = pack_weight(n((K, H)) / np.sqrt(K) / s * u.T, "e4m3")
    wd = n((H, N)) / np.sqrt(H) / u * np.exp(0.8 * n((1, N)))
    return {"tab_words": tab_words, "tab_scales": tab_scales,
            "offs": striped(np.random.permutation(T)[:S]),
            "offs2": striped(np.random.permutation(T)[:S]),
            "offs3": striped(np.random.permutation(T)[:S]),
            "w1": w1.astype(np.float32), "w2_words": w2_words, "w2_scales": w2_scales,
            "w3_words": w3_words, "w3_scales": w3_scales, "wd": wd.astype(np.float32)}

def reference(tab_words, tab_scales, offs, offs2, offs3, w1, w2_words, w2_scales, w3_words, w3_scales, wd):
    vc = unpack_weight(tab_words, tab_scales, "e4m3")[:, unstriped(offs)]
    vn = unpack_weight(tab_words, tab_scales, "e4m3")[:, unstriped(offs2)]
    vl = unpack_weight(tab_words, tab_scales, "e4m3")[:, unstriped(offs3)]
    a = mxq(f64(w1), 0, "e4m3").T @ vc
    b = unpack_weight(w2_words, w2_scales, "e2m1").T @ vn
    c = unpack_weight(w3_words, w3_scales, "e4m3").T @ vl
    d = a - b
    h = np.exp(-np.square(d)) * c
    y = mxq(f64(wd), 0, "e4m3").T @ mxq(h, 0, "e4m3")
    words, scales = planes(y)
    return y, words, scales

@@ -1,0 +1,258 @@
+from contextlib import ExitStack
+
+import concourse.mybir as mybir
+
+K, H, N, T, S = 1024, 512, 1024, 2048, 1024
+FLOPS = 2 * S * (3 * K * H + H * N)
+
+F32 = mybir.dt.float32
+BF16 = mybir.dt.bfloat16
+I32 = mybir.dt.int32
+U32 = mybir.dt.uint32
+U16 = mybir.dt.uint16
+U8 = mybir.dt.uint8
+FP8X4 = mybir.dt.float8_e4m3fn_x4
+FP4X4 = mybir.dt.float4_e2m1fn_x4
+ACT = mybir.ActivationFunctionType
+ALU = mybir.AluOpType
+
+P = 128
+PICK = 256
+COLS = 128
+WDCAST = ("scalar","scalar")
+PB = (2,2,2,2)
+GB = 2
+
+
+def YCAST(s, g):
+    return "scalar" if g == 0 and s % 2 == 0 else "vector"
+
+
+def round_copy(nc, engine, out, in_):
+    if engine == "gpsimd":
+        nc.gpsimd.tensor_scalar(out, in_, 1.0, 0.0, ALU.mult, ALU.add)
+    elif engine == "vector":
+        nc.vector.tensor_copy(out, in_)
+    else:
+        nc.scalar.copy(out, in_)
+
+
+def tile_list_ligand_affinity_response_kernel(
+    tc, tab_words, tab_scales, offs, offs2, offs3, w1, w2_words, w2_scales, w3_words, w3_scales, wd,
+    out_0, out_1, out_2,
+):
+    nc = tc.nc
+    with ExitStack() as ctx:
+        keep = ctx.enter_context(tc.tile_pool(name="keep", bufs=1))
+        picked = ctx.enter_context(tc.tile_pool(name="picked", bufs=GB))
+        work = ctx.enter_context(tc.tile_pool(name="work", bufs=3))
+        ystage = ctx.enter_context(tc.tile_pool(name="ystage", bufs=6))
+        psum = ctx.enter_context(tc.psum_pool(name="psum", bufs=2))
+
+        lists = []
+        for name, src in (("list1", offs), ("list2", offs2), ("list3", offs3)):
+            buf = keep.tile([P, S // 16], U16, name=name)
+            nc.sync.dma_start(buf[:], src)
+            lists.append(buf)
+
+        tab_sc = keep.tile([P, T], U8, name="tab_sc", align_bytes=64)
+        w_sc_raw = keep.tile([P, 3, H], U8, name="w_sc_raw", align_bytes=64)
+        nb_sc_pass1 = keep.tile([P, S], U8, name="nb_sc_pass1", align_bytes=64)
+        nc.vector.memset(tab_sc[:].bitcast(I32), 0)
+        nc.vector.memset(w_sc_raw[:].bitcast(I32), 0)
+        nc.vector.memset(nb_sc_pass1[:].bitcast(I32), 0)
+        for q in range(4):
+            nc.scalar.dma_start(
+                tab_sc[32 * q : 32 * q + 8, :].bitcast(I32), tab_scales[:, 4 * q : 4 * q + 4, :].bitcast(I32)
+            )
+        for q in range(4):
+            nc.gpsimd.dma_start(
+                w_sc_raw[32 * q : 32 * q + 4, 0:2, :].bitcast(I32),
+                w2_scales[:, 4 * q : 4 * q + 4, :].bitcast(I32).rearrange("a r e -> r a e"),
+            )
+        for q in range(4):
+            nc.gpsimd.dma_start(
+                w_sc_raw[32 * q : 32 * q + 8, 2, :].bitcast(I32), w3_scales[:, 4 * q : 4 * q + 4, :].bitcast(I32)
+            )
+
+        tab = [keep.tile([P, T], U32, name=f"tab{a}", align_bytes=64) for a in range(2)]
+        w1_raw = [keep.tile([P, 4, H], F32, name=f"w1_raw{a}") for a in range(2)]
+        w2_raw = keep.tile([P, 2, H // 2], I32, name="w2_raw")
+        w3_raw = keep.tile([P, 2, H], I32, name="w3_raw")
+        wd_raw = keep.tile([P, 4, N], F32, name="wd_raw")
+
+        def load_tab(a):
+            nc.sync.dma_start(tab[a][:].bitcast(I32), tab_words[a].rearrange("p t i -> p (t i)").bitcast(I32))
+
+        def load_w1(a):
+            nc.sync.dma_start(w1_raw[a][:], w1[512 * a : 512 * (a + 1), :].rearrange("(p j) c -> p j c", j=4))
+
+        load_tab(0)
+        load_w1(0)
+        load_w1(1)
+        load_tab(1)
+        nc.sync.dma_start(w2_raw[:], w2_words.bitcast(I32).rearrange("a p e -> p a e"))
+        nc.sync.dma_start(w3_raw[:], w3_words.rearrange("a p e i -> p a (e i)").bitcast(I32))
+        wd_rows = wd.rearrange("(b t i) n -> t b i n", t=4, i=8)
+        for t in range(4):
+            nc.sync.dma_start(wd_raw[:, t, :], wd_rows[t])
+
+        nb_sc = keep.tile([P, S], U8, name="nb_sc", align_bytes=64)
+        nc.vector.tensor_copy(nb_sc[:], tab_sc[:].indirect(lists[1][:]))
+        for q in range(4):
+            nc.scalar.dma_start(
+                nb_sc_pass1[32 * q : 32 * q + 4, :].bitcast(I32), nb_sc[32 * q + 4 : 32 * q + 8, :].bitcast(I32)
+            )
+
+        w1_codes, w1_sc = [], []
+        for a in range(2):
+            grouped = keep.tile([P, 4 * H], BF16, name=f"w1_bf{a}", align_bytes=64)
+            nc.scalar.copy(
+                grouped[:].rearrange("p (t b i j) -> p t b i j", t=4, i=8, j=4),
+                w1_raw[a][:].rearrange("p j (b t i) -> p t b i j", t=4, i=8),
+            )
+            codes = keep.tile([P, H], U32, name=f"w1_codes{a}", align_bytes=64)
+            sc = keep.tile([P, H], U8, name=f"w1_sc{a}", align_bytes=64)
+            nc.vector.quantize_mx(codes[:].bitcast(FP8X4), sc[:], grouped[:])
+            w1_codes.append(codes)
+            w1_sc.append(sc)
+
+        w2_codes = keep.tile([P, 2, 2 * H], U8, name="w2_codes", align_bytes=64)
+        w3_codes = keep.tile([P, 2, H], U32, name="w3_codes", align_bytes=64)
+        w_sc = keep.tile([P, 3, H], U8, name="w_sc", align_bytes=64)
+        nc.gpsimd.tensor_copy(
+            w_sc[:].bitcast(I32).rearrange("p x (t b w) -> p x t b w", t=4, w=2),
+            w_sc_raw[:].bitcast(I32).rearrange("p x (b t w) -> p x t b w", t=4, w=2),
+        )
+        nc.gpsimd.tensor_copy(
+            w2_codes[:].bitcast(I32).rearrange("p a (t b w) -> p a t b w", t=4, w=4),
+            w2_raw[:].rearrange("p a (b t w) -> p a t b w", t=4, w=4),
+        )
+        for a in range(2):
+            nc.gpsimd.tensor_copy(
+                w3_codes[:, a, :].bitcast(I32).rearrange("p (t b w) -> p t b w", t=4, w=8),
+                w3_raw[:, a, :].rearrange("p (b t w) -> p t b w", t=4, w=8),
+            )
+
+        wd_codes, wd_sc = [], []
+
+        def prepare_wd(g):
+            grouped = keep.tile([P, 4 * 512], BF16, name=f"wd_bf{g}", align_bytes=64)
+            dst = grouped[:].rearrange("p (u m t) -> p m u t", u=4, t=4)
+            src = wd_raw[:, :, 512 * g : 512 * (g + 1)].rearrange("p t (m u) -> p m u t", u=4)
+            for m0 in range(0, P, 32):
+                round_copy(nc, WDCAST[g], dst[:, m0 : m0 + 32], src[:, m0 : m0 + 32])
+            codes = keep.tile([P, 512], U32, name=f"wd_codes{g}", align_bytes=64)
+            sc = keep.tile([P, 512], U8, name=f"wd_sc{g}", align_bytes=64)
+            nc.vector.quantize_mx(codes[:].bitcast(FP8X4), sc[:], grouped[:])
+            wd_codes.append(codes)
+            wd_sc.append(sc)
+
+        y_sc = keep.tile([P, 2, S], U8, name="y_sc", align_bytes=64)
+        y_rows = out_0.rearrange("(g p u) j -> g p u j", g=2, u=4)
+        y_words = out_1.rearrange("g p m t -> p g (m t)").bitcast(I32)
+
+        def gather(c):
+            cols = slice(c * PICK // 16, (c + 1) * PICK // 16)
+            words = [[None, None] for x in range(3)]
+            scales = [None, None, None]
+            for a in range(2):
+                for x in range(3):
+                    buf = picked.tile([P, PICK], U32, name=f"words{x}{a}", align_bytes=64)
+                    nc.vector.tensor_copy(buf[:], tab[a][:].indirect(lists[x][:, cols]))
+                    words[x][a] = buf
+                    if a == 0 and x != 1:
+                        buf = picked.tile([P, PICK], U8, name=f"scales{x}", align_bytes=64)
+                        nc.vector.tensor_copy(buf[:], tab_sc[:].indirect(lists[x][:, cols]))
+                        scales[x] = buf
+            return words, scales
+
+        def first_stage(s, words, scales):
+            cols = slice(s * COLS % PICK, s * COLS % PICK + COLS)
+            whole = slice(s * COLS, (s + 1) * COLS)
+            a_ps = psum.tile([P, 4, COLS], F32, name="a_ps", bufs=PB[0])
+            b_ps = psum.tile([P, 4, COLS], F32, name="b_ps", bufs=PB[1])
+            c_ps = psum.tile([P, 4, COLS], F32, name="c_ps", bufs=PB[2])
+            for t in range(4):
+                rows = slice(P * t, P * (t + 1))
+                for a in range(2):
+                    nc.tensor.matmul_mx(
+                        a_ps[:, t, :],
+                        lhsT=w1_codes[a][:, rows].bitcast(FP8X4), lhsT_scale=w1_sc[a][:, rows],
+                        rhs=words[0][a][:, cols].bitcast(FP8X4), rhs_scale=scales[0][4 * a :, cols],
+                        start=a == 0, stop=a == 1,
+                    )
+            for t in range(4):
+                rows = slice(P * t, P * (t + 1))
+                for a in range(2):
+                    nc.tensor.matmul_mx(
+                        b_ps[:, t, :],
+                        lhsT=w2_codes[:, a, 2 * P * t : 2 * P * (t + 1)].bitcast(FP4X4), lhsT_scale=w_sc[:, a, rows],
+                        rhs=words[1][a][:, cols].bitcast(FP8X4), rhs_scale=(nb_sc, nb_sc_pass1)[a][:, whole],
+                        start=a == 0, stop=a == 1,
+                    )
+            for t in range(4):
+                rows = slice(P * t, P * (t + 1))
+                for a in range(2):
+                    nc.tensor.matmul_mx(
+                        c_ps[:, t, :],
+                        lhsT=w3_codes[:, a, rows].bitcast(FP8X4), lhsT_scale=w_sc[4 * a :, 2, rows],
+                        rhs=words[2][a][:, cols].bitcast(FP8X4), rhs_scale=scales[2][4 * a :, cols],
+                        start=a == 0, stop=a == 1,
+                    )
+            a_sb = work.tile([P, COLS, 4], F32, name="a_sb")
+            nc.scalar.copy(a_sb[:], a_ps[:].rearrange("p t j -> p j t"))
+            diff = work.tile([P, COLS, 4], F32, name="diff")
+            nc.vector.tensor_tensor(diff[:], a_sb[:], b_ps[:].rearrange("p t j -> p j t"), ALU.subtract)
+            square = work.tile([P, COLS, 4], F32, name="square")
+            nc.scalar.activation(square[:], diff[:], ACT.Square)
+            affinity = work.tile([P, COLS, 4], F32, name="affinity")
+            nc.scalar.activation(affinity[:], square[:], ACT.Exp, scale=-1.0)
+            h_bf = work.tile([P, COLS, 4], BF16, name="h_bf", align_bytes=64)
+            nc.vector.tensor_tensor(h_bf[:], affinity[:], c_ps[:].rearrange("p t j -> p j t"), ALU.mult)
+            h_codes = work.tile([P, COLS], U32, name="h_codes", align_bytes=64, bufs=8)
+            h_sc = work.tile([P, COLS], U8, name="h_sc", align_bytes=64, bufs=8)
+            nc.vector.quantize_mx(h_codes[:].bitcast(FP8X4), h_sc[:], h_bf[:].rearrange("p j t -> p (j t)"))
+            return h_codes, h_sc
+
+        def second_stage(s, h_codes, h_sc):
+            whole = slice(s * COLS, (s + 1) * COLS)
+            y_codes = ystage.tile([P, 2, COLS], U32, name="y_codes", align_bytes=64)
+            for g in range(2):
+                y_ps = psum.tile([P, 4, COLS], F32, name="y_ps", bufs=PB[3])
+                for u in range(4):
+                    rows = slice(P * u, P * (u + 1))
+                    nc.tensor.matmul_mx(
+                        y_ps[:, u, :],
+                        lhsT=wd_codes[g][:, rows].bitcast(FP8X4), lhsT_scale=wd_sc[g][:, rows],
+                        rhs=h_codes[:].bitcast(FP8X4), rhs_scale=h_sc[:],
+                        start=True, stop=True,
+                    )
+                y_sb = ystage.tile([P, 4, COLS], F32, name="y_sb")
+                nc.scalar.copy(y_sb[:], y_ps[:])
+                nc.sync.dma_start(y_rows[g][:, :, whole], y_sb[:])
+                y_bf = ystage.tile([P, COLS, 4], BF16, name="y_bf", align_bytes=64)
+                engine = YCAST(s, g)
+                source = y_ps if engine == "scalar" else y_sb
+                round_copy(nc, engine, y_bf[:], source[:].rearrange("p u j -> p j u"))
+                nc.vector.quantize_mx(
+                    y_codes[:, g, :].bitcast(FP8X4), y_sc[:, g, whole], y_bf[:].rearrange("p j u -> p (j u)")
+                )
+            nc.sync.dma_start(y_words[:, :, whole], y_codes[:].bitcast(I32))
+
+        steps = S // COLS
+        for s in range(steps):
+            if s * COLS % PICK == 0:
+                words, scales = gather(s * COLS // PICK)
+            h_codes, h_sc = first_stage(s, words, scales)
+            if s == 0:
+                prepare_wd(0)
+                prepare_wd(1)
+            second_stage(s, h_codes, h_sc)
+
+        for q in range(4):
+            engine = nc.sync if q % 2 == 0 else nc.scalar
+            engine.dma_start(
+                out_2[:, 4 * q : 4 * q + 4, :].bitcast(I32).rearrange("g r m -> r g m"),
+                y_sc[32 * q : 32 * q + 4, :, :].bitcast(I32),
+            )

@@ -19,13 +19,13 @@ ALU = mybir.AluOpType
 P = 128
 PICK = 256
 COLS = 128
-WDCAST = ("scalar","scalar")
+WDCAST = ("gpsimd","gpsimd")
+HELD = 4
 PB = (2,2,2,2)
-GB = 2
 
 
 def YCAST(s, g):
-    return "scalar" if g == 0 and s % 2 == 0 else "vector"
+    return "gpsimd"
 
 
 def round_copy(nc, engine, out, in_):
@@ -44,8 +44,7 @@ def tile_list_ligand_affinity_response_kernel(
     nc = tc.nc
     with ExitStack() as ctx:
         keep = ctx.enter_context(tc.tile_pool(name="keep", bufs=1))
-        picked = ctx.enter_context(tc.tile_pool(name="picked", bufs=GB))
-        work = ctx.enter_context(tc.tile_pool(name="work", bufs=3))
+        work = ctx.enter_context(tc.tile_pool(name="work", bufs=2))
         ystage = ctx.enter_context(tc.tile_pool(name="ystage", bufs=6))
         psum = ctx.enter_context(tc.psum_pool(name="psum", bufs=2))
 
@@ -79,7 +78,12 @@ def tile_list_ligand_affinity_response_kernel(
         w1_raw = [keep.tile([P, 4, H], F32, name=f"w1_raw{a}") for a in range(2)]
         w2_raw = keep.tile([P, 2, H // 2], I32, name="w2_raw")
         w3_raw = keep.tile([P, 2, H], I32, name="w3_raw")
-        wd_raw = keep.tile([P, 4, N], F32, name="wd_raw")
+        wd_raw = [keep.tile([P, 4, 512], F32, name=f"wd_raw{g}") for g in range(2)]
+        wd_rows = wd.rearrange("(b t i) n -> t b i n", t=4, i=8)
+
+        def load_wd(g):
+            for t in range(4):
+                nc.sync.dma_start(wd_raw[g][:, t, :], wd_rows[t][:, :, 512 * g : 512 * (g + 1)])
 
         def load_tab(a):
             nc.sync.dma_start(tab[a][:].bitcast(I32), tab_words[a].rearrange("p t i -> p (t i)").bitcast(I32))
@@ -88,14 +92,13 @@ def tile_list_ligand_affinity_response_kernel(
             nc.sync.dma_start(w1_raw[a][:], w1[512 * a : 512 * (a + 1), :].rearrange("(p j) c -> p j c", j=4))
 
         load_tab(0)
+        nc.sync.dma_start(w2_raw[:], w2_words.bitcast(I32).rearrange("a p e -> p a e"))
+        nc.sync.dma_start(w3_raw[:], w3_words.rearrange("a p e i -> p a (e i)").bitcast(I32))
         load_w1(0)
         load_w1(1)
         load_tab(1)
-        nc.sync.dma_start(w2_raw[:], w2_words.bitcast(I32).rearrange("a p e -> p a e"))
-        nc.sync.dma_start(w3_raw[:], w3_words.rearrange("a p e i -> p a (e i)").bitcast(I32))
-        wd_rows = wd.rearrange("(b t i) n -> t b i n", t=4, i=8)
-        for t in range(4):
-            nc.sync.dma_start(wd_raw[:, t, :], wd_rows[t])
+        load_wd(0)
+        load_wd(1)
 
         nb_sc = keep.tile([P, S], U8, name="nb_sc", align_bytes=64)
         nc.vector.tensor_copy(nb_sc[:], tab_sc[:].indirect(lists[1][:]))
@@ -120,26 +123,27 @@ def tile_list_ligand_affinity_response_kernel(
         w2_codes = keep.tile([P, 2, 2 * H], U8, name="w2_codes", align_bytes=64)
         w3_codes = keep.tile([P, 2, H], U32, name="w3_codes", align_bytes=64)
         w_sc = keep.tile([P, 3, H], U8, name="w_sc", align_bytes=64)
+        nc.scalar.copy(
+            w2_codes[:].bitcast(U32).rearrange("p a (t b w) -> p a t b w", t=4, w=4),
+            w2_raw[:].bitcast(U32).rearrange("p a (b t w) -> p a t b w", t=4, w=4),
+        )
+        for a in range(2):
+            nc.scalar.copy(
+                w3_codes[:, a, :].rearrange("p (t b w) -> p t b w", t=4, w=8),
+                w3_raw[:, a, :].bitcast(U32).rearrange("p (b t w) -> p t b w", t=4, w=8),
+            )
+
         nc.gpsimd.tensor_copy(
             w_sc[:].bitcast(I32).rearrange("p x (t b w) -> p x t b w", t=4, w=2),
             w_sc_raw[:].bitcast(I32).rearrange("p x (b t w) -> p x t b w", t=4, w=2),
         )
-        nc.gpsimd.tensor_copy(
-            w2_codes[:].bitcast(I32).rearrange("p a (t b w) -> p a t b w", t=4, w=4),
-            w2_raw[:].rearrange("p a (b t w) -> p a t b w", t=4, w=4),
-        )
-        for a in range(2):
-            nc.gpsimd.tensor_copy(
-                w3_codes[:, a, :].bitcast(I32).rearrange("p (t b w) -> p t b w", t=4, w=8),
-                w3_raw[:, a, :].rearrange("p (b t w) -> p t b w", t=4, w=8),
-            )
 
         wd_codes, wd_sc = [], []
 
         def prepare_wd(g):
             grouped = keep.tile([P, 4 * 512], BF16, name=f"wd_bf{g}", align_bytes=64)
             dst = grouped[:].rearrange("p (u m t) -> p m u t", u=4, t=4)
-            src = wd_raw[:, :, 512 * g : 512 * (g + 1)].rearrange("p t (m u) -> p m u t", u=4)
+            src = wd_raw[g][:].rearrange("p t (m u) -> p m u t", u=4)
             for m0 in range(0, P, 32):
                 round_copy(nc, WDCAST[g], dst[:, m0 : m0 + 32], src[:, m0 : m0 + 32])
             codes = keep.tile([P, 512], U32, name=f"wd_codes{g}", align_bytes=64)
@@ -152,22 +156,28 @@ def tile_list_ligand_affinity_response_kernel(
         y_rows = out_0.rearrange("(g p u) j -> g p u j", g=2, u=4)
         y_words = out_1.rearrange("g p m t -> p g (m t)").bitcast(I32)
 
-        def gather(c):
-            cols = slice(c * PICK // 16, (c + 1) * PICK // 16)
-            words = [[None, None] for x in range(3)]
-            scales = [None, None, None]
-            for a in range(2):
-                for x in range(3):
-                    buf = picked.tile([P, PICK], U32, name=f"words{x}{a}", align_bytes=64)
-                    nc.vector.tensor_copy(buf[:], tab[a][:].indirect(lists[x][:, cols]))
-                    words[x][a] = buf
-                    if a == 0 and x != 1:
-                        buf = picked.tile([P, PICK], U8, name=f"scales{x}", align_bytes=64)
-                        nc.vector.tensor_copy(buf[:], tab_sc[:].indirect(lists[x][:, cols]))
-                        scales[x] = buf
-            return words, scales
+        words, scales = {}, {}
 
-        def first_stage(s, words, scales):
+        def gather(c, x, a, tag):
+            cols = slice(c * PICK // 16, (c + 1) * PICK // 16)
+            if a is None:
+                buf = keep.tile([P, PICK], U8, name=f"scales{c}{x}", tag=tag, align_bytes=64)
+                nc.vector.tensor_copy(buf[:], tab_sc[:].indirect(lists[x][:, cols]))
+                scales[c, x] = buf
+            else:
+                buf = keep.tile([P, PICK], U32, name=f"words{c}{x}{a}", tag=tag, align_bytes=64)
+                nc.vector.tensor_copy(buf[:], tab[a][:].indirect(lists[x][:, cols]))
+                words[c, x, a] = buf
+
+        per_chunk = [(0, 0), (0, None), (0, 1), (1, 0), (1, 1), (2, 0), (2, None), (2, 1)]
+        early = [(c, x, a) for c in range(2) for x, a in per_chunk if a != 1] + [(0, x, 1) for x in range(3)]
+        late = [(c, x, a) for c in range(S // PICK) for x, a in per_chunk if (c, x, a) not in early]
+        slots = [(0, k) for k in ("a_sb", "diff", "square")] + [(s, k) for s in range(1, 5) for k in ("a_sb", "diff", "square", "affinity")]
+        for c, x, a in early:
+            gather(c, x, a, f"early{c}{x}{a}")
+
+        def first_stage(s):
+            c = s * COLS // PICK
             cols = slice(s * COLS % PICK, s * COLS % PICK + COLS)
             whole = slice(s * COLS, (s + 1) * COLS)
             a_ps = psum.tile([P, 4, COLS], F32, name="a_ps", bufs=PB[0])
@@ -179,7 +189,7 @@ def tile_list_ligand_affinity_response_kernel(
                     nc.tensor.matmul_mx(
                         a_ps[:, t, :],
                         lhsT=w1_codes[a][:, rows].bitcast(FP8X4), lhsT_scale=w1_sc[a][:, rows],
-                        rhs=words[0][a][:, cols].bitcast(FP8X4), rhs_scale=scales[0][4 * a :, cols],
+                        rhs=words[c, 0, a][:, cols].bitcast(FP8X4), rhs_scale=scales[c, 0][4 * a :, cols],
                         start=a == 0, stop=a == 1,
                     )
             for t in range(4):
@@ -188,7 +198,7 @@ def tile_list_ligand_affinity_response_kernel(
                     nc.tensor.matmul_mx(
                         b_ps[:, t, :],
                         lhsT=w2_codes[:, a, 2 * P * t : 2 * P * (t + 1)].bitcast(FP4X4), lhsT_scale=w_sc[:, a, rows],
-                        rhs=words[1][a][:, cols].bitcast(FP8X4), rhs_scale=(nb_sc, nb_sc_pass1)[a][:, whole],
+                        rhs=words[c, 1, a][:, cols].bitcast(FP8X4), rhs_scale=(nb_sc, nb_sc_pass1)[a][:, whole],
                         start=a == 0, stop=a == 1,
                     )
             for t in range(4):
@@ -197,21 +207,21 @@ def tile_list_ligand_affinity_response_kernel(
                     nc.tensor.matmul_mx(
                         c_ps[:, t, :],
                         lhsT=w3_codes[:, a, rows].bitcast(FP8X4), lhsT_scale=w_sc[4 * a :, 2, rows],
-                        rhs=words[2][a][:, cols].bitcast(FP8X4), rhs_scale=scales[2][4 * a :, cols],
+                        rhs=words[c, 2, a][:, cols].bitcast(FP8X4), rhs_scale=scales[c, 2][4 * a :, cols],
                         start=a == 0, stop=a == 1,
                     )
-            a_sb = work.tile([P, COLS, 4], F32, name="a_sb")
+            a_sb = keep.tile([P, COLS, 4], F32, name="a_sb", tag=f"a_sb{s}", align_bytes=64)
             nc.scalar.copy(a_sb[:], a_ps[:].rearrange("p t j -> p j t"))
-            diff = work.tile([P, COLS, 4], F32, name="diff")
+            diff = keep.tile([P, COLS, 4], F32, name="diff", tag=f"diff{s}", align_bytes=64)
             nc.vector.tensor_tensor(diff[:], a_sb[:], b_ps[:].rearrange("p t j -> p j t"), ALU.subtract)
-            square = work.tile([P, COLS, 4], F32, name="square")
+            square = keep.tile([P, COLS, 4], F32, name="square", tag=f"square{s}", align_bytes=64)
             nc.scalar.activation(square[:], diff[:], ACT.Square)
-            affinity = work.tile([P, COLS, 4], F32, name="affinity")
+            affinity = keep.tile([P, COLS, 4], F32, name="affinity", tag=f"affinity{s}", align_bytes=64)
             nc.scalar.activation(affinity[:], square[:], ACT.Exp, scale=-1.0)
-            h_bf = work.tile([P, COLS, 4], BF16, name="h_bf", align_bytes=64)
+            h_bf = keep.tile([P, COLS, 4], BF16, name="h_bf", tag=f"diff{s + 1}" if s < HELD else f"h_bf{s}", align_bytes=64)
             nc.vector.tensor_tensor(h_bf[:], affinity[:], c_ps[:].rearrange("p t j -> p j t"), ALU.mult)
-            h_codes = work.tile([P, COLS], U32, name="h_codes", align_bytes=64, bufs=8)
-            h_sc = work.tile([P, COLS], U8, name="h_sc", align_bytes=64, bufs=8)
+            h_codes = work.tile([P, COLS], U32, name="h_codes", align_bytes=64, bufs=3)
+            h_sc = work.tile([P, COLS], U8, name="h_sc", align_bytes=64, bufs=3)
             nc.vector.quantize_mx(h_codes[:].bitcast(FP8X4), h_sc[:], h_bf[:].rearrange("p j t -> p (j t)"))
             return h_codes, h_sc
 
@@ -242,9 +252,10 @@ def tile_list_ligand_affinity_response_kernel(
 
         steps = S // COLS
         for s in range(steps):
-            if s * COLS % PICK == 0:
-                words, scales = gather(s * COLS // PICK)
-            h_codes, h_sc = first_stage(s, words, scales)
+            h_codes, h_sc = first_stage(s)
+            for (step, kind), (c, x, a) in zip(slots, late):
+                if step == s:
+                    gather(c, x, a, f"{kind}{s}")
             if s == 0:
                 prepare_wd(0)
                 prepare_wd(1)

@@ -19,22 +19,10 @@ ALU = mybir.AluOpType
 P = 128
 PICK = 256
 COLS = 128
-WDCAST = ("gpsimd","gpsimd")
-HELD = 4
-PB = (2,2,2,2)
-
-
-def YCAST(s, g):
-    return "gpsimd"
-
-
-def round_copy(nc, engine, out, in_):
-    if engine == "gpsimd":
-        nc.gpsimd.tensor_scalar(out, in_, 1.0, 0.0, ALU.mult, ALU.add)
-    elif engine == "vector":
-        nc.vector.tensor_copy(out, in_)
-    else:
-        nc.scalar.copy(out, in_)
+STEPS = S // COLS
+LAG = 2
+ROUNDED_ON_SCALAR = 2
+DONORS = ("a_sb", "diff")
 
 
 def tile_list_ligand_affinity_response_kernel(
@@ -44,7 +32,7 @@ def tile_list_ligand_affinity_response_kernel(
     nc = tc.nc
     with ExitStack() as ctx:
         keep = ctx.enter_context(tc.tile_pool(name="keep", bufs=1))
-        work = ctx.enter_context(tc.tile_pool(name="work", bufs=2))
+        hstage = ctx.enter_context(tc.tile_pool(name="hstage", bufs=3))
         ystage = ctx.enter_context(tc.tile_pool(name="ystage", bufs=6))
         psum = ctx.enter_context(tc.psum_pool(name="psum", bufs=2))
 
@@ -55,23 +43,21 @@ def tile_list_ligand_affinity_response_kernel(
             lists.append(buf)
 
         tab_sc = keep.tile([P, T], U8, name="tab_sc", align_bytes=64)
-        w_sc_raw = keep.tile([P, 3, H], U8, name="w_sc_raw", align_bytes=64)
+        w2_sc_raw = keep.tile([P, 2 * H], U8, name="w2_sc_raw")
+        w3_sc_raw = keep.tile([P, H], U8, name="w3_sc_raw")
         nb_sc_pass1 = keep.tile([P, S], U8, name="nb_sc_pass1", align_bytes=64)
         nc.vector.memset(tab_sc[:].bitcast(I32), 0)
-        nc.vector.memset(w_sc_raw[:].bitcast(I32), 0)
+        nc.vector.memset(w2_sc_raw[:].bitcast(I32), 0)
         nc.vector.memset(nb_sc_pass1[:].bitcast(I32), 0)
+        nc.vector.memset(w3_sc_raw[:].bitcast(I32), 0)
         for q in range(4):
             nc.scalar.dma_start(
                 tab_sc[32 * q : 32 * q + 8, :].bitcast(I32), tab_scales[:, 4 * q : 4 * q + 4, :].bitcast(I32)
             )
         for q in range(4):
-            nc.gpsimd.dma_start(
-                w_sc_raw[32 * q : 32 * q + 4, 0:2, :].bitcast(I32),
+            nc.scalar.dma_start(
+                w2_sc_raw[32 * q : 32 * q + 4, :].bitcast(I32).rearrange("r (a e) -> r a e", a=2),
                 w2_scales[:, 4 * q : 4 * q + 4, :].bitcast(I32).rearrange("a r e -> r a e"),
-            )
-        for q in range(4):
-            nc.gpsimd.dma_start(
-                w_sc_raw[32 * q : 32 * q + 8, 2, :].bitcast(I32), w3_scales[:, 4 * q : 4 * q + 4, :].bitcast(I32)
             )
 
         tab = [keep.tile([P, T], U32, name=f"tab{a}", align_bytes=64) for a in range(2)]
@@ -91,38 +77,50 @@ def tile_list_ligand_affinity_response_kernel(
         def load_w1(a):
             nc.sync.dma_start(w1_raw[a][:], w1[512 * a : 512 * (a + 1), :].rearrange("(p j) c -> p j c", j=4))
 
+        def load_w23():
+            nc.sync.dma_start(w2_raw[:], w2_words.bitcast(I32).rearrange("a p e -> p a e"))
+            nc.sync.dma_start(w3_raw[:], w3_words.rearrange("a p e i -> p a (e i)").bitcast(I32))
+
         load_tab(0)
-        nc.sync.dma_start(w2_raw[:], w2_words.bitcast(I32).rearrange("a p e -> p a e"))
-        nc.sync.dma_start(w3_raw[:], w3_words.rearrange("a p e i -> p a (e i)").bitcast(I32))
         load_w1(0)
         load_w1(1)
-        load_tab(1)
+
+        picked_sc = [None, None, None]
+        for x in (1, 0, 2):
+            buf = keep.tile([P, S], U8, name=f"picked_sc{x}", align_bytes=64)
+            nc.vector.tensor_copy(buf[:], tab_sc[:].indirect(lists[x][:]))
+            picked_sc[x] = buf
+        for q in range(4):
+            nc.sync.dma_start(
+                nb_sc_pass1[32 * q : 32 * q + 4, :].bitcast(I32),
+                picked_sc[1][32 * q + 4 : 32 * q + 8, :].bitcast(I32),
+            )
+
+        load_w23()
         load_wd(0)
         load_wd(1)
-
-        nb_sc = keep.tile([P, S], U8, name="nb_sc", align_bytes=64)
-        nc.vector.tensor_copy(nb_sc[:], tab_sc[:].indirect(lists[1][:]))
+        load_tab(1)
         for q in range(4):
-            nc.scalar.dma_start(
-                nb_sc_pass1[32 * q : 32 * q + 4, :].bitcast(I32), nb_sc[32 * q + 4 : 32 * q + 8, :].bitcast(I32)
+            nc.sync.dma_start(
+                w3_sc_raw[32 * q : 32 * q + 8, :].bitcast(I32), w3_scales[:, 4 * q : 4 * q + 4, :].bitcast(I32)
             )
 
         w1_codes, w1_sc = [], []
         for a in range(2):
-            grouped = keep.tile([P, 4 * H], BF16, name=f"w1_bf{a}", align_bytes=64)
-            nc.scalar.copy(
-                grouped[:].rearrange("p (t b i j) -> p t b i j", t=4, i=8, j=4),
-                w1_raw[a][:].rearrange("p j (b t i) -> p t b i j", t=4, i=8),
-            )
+            grouped = keep.tile([P, 4, 4 * P], BF16, name=f"w1_bf{a}", align_bytes=64)
+            source = w1_raw[a][:].rearrange("p j (b t h i) -> p t b h j i", t=4, h=2, i=4)
+            for t in range(4):
+                nc.scalar.copy(grouped[:, t, :].rearrange("p (b h i j) -> p b h j i", h=2, i=4, j=4), source[:, t])
             codes = keep.tile([P, H], U32, name=f"w1_codes{a}", align_bytes=64)
             sc = keep.tile([P, H], U8, name=f"w1_sc{a}", align_bytes=64)
-            nc.vector.quantize_mx(codes[:].bitcast(FP8X4), sc[:], grouped[:])
+            nc.vector.quantize_mx(codes[:].bitcast(FP8X4), sc[:], grouped[:].rearrange("p t e -> p (t e)"))
             w1_codes.append(codes)
             w1_sc.append(sc)
 
         w2_codes = keep.tile([P, 2, 2 * H], U8, name="w2_codes", align_bytes=64)
         w3_codes = keep.tile([P, 2, H], U32, name="w3_codes", align_bytes=64)
-        w_sc = keep.tile([P, 3, H], U8, name="w_sc", align_bytes=64)
+        w2_sc = keep.tile([P, 2, H], U8, name="w2_sc", align_bytes=64)
+        w3_sc = keep.tile([P, H], U8, name="w3_sc", align_bytes=64)
         nc.scalar.copy(
             w2_codes[:].bitcast(U32).rearrange("p a (t b w) -> p a t b w", t=4, w=4),
             w2_raw[:].bitcast(U32).rearrange("p a (b t w) -> p a t b w", t=4, w=4),
@@ -132,64 +130,72 @@ def tile_list_ligand_affinity_response_kernel(
                 w3_codes[:, a, :].rearrange("p (t b w) -> p t b w", t=4, w=8),
                 w3_raw[:, a, :].bitcast(U32).rearrange("p (b t w) -> p t b w", t=4, w=8),
             )
-
-        nc.gpsimd.tensor_copy(
-            w_sc[:].bitcast(I32).rearrange("p x (t b w) -> p x t b w", t=4, w=2),
-            w_sc_raw[:].bitcast(I32).rearrange("p x (b t w) -> p x t b w", t=4, w=2),
+        nc.scalar.copy(
+            w2_sc[:].bitcast(U32).rearrange("p a (t b w) -> p a t b w", t=4, w=2),
+            w2_sc_raw[:].bitcast(U32).rearrange("p (a b t w) -> p a t b w", a=2, t=4, w=2),
+        )
+        nc.scalar.copy(
+            w3_sc[:].bitcast(U32).rearrange("p (t b w) -> p t b w", t=4, w=2),
+            w3_sc_raw[:].bitcast(U32).rearrange("p (b t w) -> p t b w", t=4, w=2),
         )
 
-        wd_codes, wd_sc = [], []
+        first_words = []
+        for x in range(3):
+            buf = keep.tile([P, S], U32, name=f"first_words{x}", align_bytes=64)
+            nc.vector.tensor_copy(buf[:], tab[0][:].indirect(lists[x][:]))
+            first_words.append(buf)
 
-        def prepare_wd(g):
+        wd_bf, wd_codes, wd_sc = [], [], []
+        for g in range(2):
             grouped = keep.tile([P, 4 * 512], BF16, name=f"wd_bf{g}", align_bytes=64)
-            dst = grouped[:].rearrange("p (u m t) -> p m u t", u=4, t=4)
-            src = wd_raw[g][:].rearrange("p t (m u) -> p m u t", u=4)
+            dst = grouped[:].rearrange("p (u m t) -> p m t u", u=4, t=4)
+            src = wd_raw[g][:].rearrange("p t (m u) -> p m t u", u=4)
             for m0 in range(0, P, 32):
-                round_copy(nc, WDCAST[g], dst[:, m0 : m0 + 32], src[:, m0 : m0 + 32])
-            codes = keep.tile([P, 512], U32, name=f"wd_codes{g}", align_bytes=64)
+                nc.scalar.copy(dst[:, m0 : m0 + 32], src[:, m0 : m0 + 32])
+            wd_bf.append(grouped)
+
+        def quantise_wd(g, tag):
+            codes = keep.tile([P, 512], U32, name=f"wd_codes{g}", tag=tag, align_bytes=64)
             sc = keep.tile([P, 512], U8, name=f"wd_sc{g}", align_bytes=64)
-            nc.vector.quantize_mx(codes[:].bitcast(FP8X4), sc[:], grouped[:])
+            nc.vector.quantize_mx(codes[:].bitcast(FP8X4), sc[:], wd_bf[g][:])
             wd_codes.append(codes)
             wd_sc.append(sc)
+
+        quantise_wd(0, "wd_codes0")
+
+        second_words = {}
+
+        def gather_second(c, x, tag):
+            buf = keep.tile([P, PICK], U32, name=f"second_words{c}{x}", tag=tag, align_bytes=64)
+            nc.vector.tensor_copy(buf[:], tab[1][:].indirect(lists[x][:, c * PICK // 16 : (c + 1) * PICK // 16]))
+            second_words[c, x] = buf
+
+        for x in range(3):
+            gather_second(0, x, f"second_words{x}")
+        late = [(c, x) for c in range(1, S // PICK) for x in range(3)]
 
         y_sc = keep.tile([P, 2, S], U8, name="y_sc", align_bytes=64)
         y_rows = out_0.rearrange("(g p u) j -> g p u j", g=2, u=4)
         y_words = out_1.rearrange("g p m t -> p g (m t)").bitcast(I32)
 
-        words, scales = {}, {}
-
-        def gather(c, x, a, tag):
-            cols = slice(c * PICK // 16, (c + 1) * PICK // 16)
-            if a is None:
-                buf = keep.tile([P, PICK], U8, name=f"scales{c}{x}", tag=tag, align_bytes=64)
-                nc.vector.tensor_copy(buf[:], tab_sc[:].indirect(lists[x][:, cols]))
-                scales[c, x] = buf
-            else:
-                buf = keep.tile([P, PICK], U32, name=f"words{c}{x}{a}", tag=tag, align_bytes=64)
-                nc.vector.tensor_copy(buf[:], tab[a][:].indirect(lists[x][:, cols]))
-                words[c, x, a] = buf
-
-        per_chunk = [(0, 0), (0, None), (0, 1), (1, 0), (1, 1), (2, 0), (2, None), (2, 1)]
-        early = [(c, x, a) for c in range(2) for x, a in per_chunk if a != 1] + [(0, x, 1) for x in range(3)]
-        late = [(c, x, a) for c in range(S // PICK) for x, a in per_chunk if (c, x, a) not in early]
-        slots = [(0, k) for k in ("a_sb", "diff", "square")] + [(s, k) for s in range(1, 5) for k in ("a_sb", "diff", "square", "affinity")]
-        for c, x, a in early:
-            gather(c, x, a, f"early{c}{x}{a}")
-
         def first_stage(s):
-            c = s * COLS // PICK
-            cols = slice(s * COLS % PICK, s * COLS % PICK + COLS)
             whole = slice(s * COLS, (s + 1) * COLS)
-            a_ps = psum.tile([P, 4, COLS], F32, name="a_ps", bufs=PB[0])
-            b_ps = psum.tile([P, 4, COLS], F32, name="b_ps", bufs=PB[1])
-            c_ps = psum.tile([P, 4, COLS], F32, name="c_ps", bufs=PB[2])
+            within = slice(s * COLS % PICK, s * COLS % PICK + COLS)
+
+            def moving(x, a):
+                words = first_words[x][:, whole] if a == 0 else second_words[s * COLS // PICK, x][:, within]
+                return words.bitcast(FP8X4)
+
+            a_ps = psum.tile([P, 4, COLS], F32, name="a_ps")
+            b_ps = psum.tile([P, 4, COLS], F32, name="b_ps")
+            c_ps = psum.tile([P, 4, COLS], F32, name="c_ps")
             for t in range(4):
                 rows = slice(P * t, P * (t + 1))
                 for a in range(2):
                     nc.tensor.matmul_mx(
                         a_ps[:, t, :],
                         lhsT=w1_codes[a][:, rows].bitcast(FP8X4), lhsT_scale=w1_sc[a][:, rows],
-                        rhs=words[c, 0, a][:, cols].bitcast(FP8X4), rhs_scale=scales[c, 0][4 * a :, cols],
+                        rhs=moving(0, a), rhs_scale=picked_sc[0][4 * a :, whole],
                         start=a == 0, stop=a == 1,
                     )
             for t in range(4):
@@ -197,8 +203,8 @@ def tile_list_ligand_affinity_response_kernel(
                 for a in range(2):
                     nc.tensor.matmul_mx(
                         b_ps[:, t, :],
-                        lhsT=w2_codes[:, a, 2 * P * t : 2 * P * (t + 1)].bitcast(FP4X4), lhsT_scale=w_sc[:, a, rows],
-                        rhs=words[c, 1, a][:, cols].bitcast(FP8X4), rhs_scale=(nb_sc, nb_sc_pass1)[a][:, whole],
+                        lhsT=w2_codes[:, a, 2 * P * t : 2 * P * (t + 1)].bitcast(FP4X4), lhsT_scale=w2_sc[:, a, rows],
+                        rhs=moving(1, a), rhs_scale=(picked_sc[1], nb_sc_pass1)[a][:, whole],
                         start=a == 0, stop=a == 1,
                     )
             for t in range(4):
@@ -206,8 +212,8 @@ def tile_list_ligand_affinity_response_kernel(
                 for a in range(2):
                     nc.tensor.matmul_mx(
                         c_ps[:, t, :],
-                        lhsT=w3_codes[:, a, rows].bitcast(FP8X4), lhsT_scale=w_sc[4 * a :, 2, rows],
-                        rhs=words[c, 2, a][:, cols].bitcast(FP8X4), rhs_scale=scales[c, 2][4 * a :, cols],
+                        lhsT=w3_codes[:, a, rows].bitcast(FP8X4), lhsT_scale=w3_sc[4 * a :, rows],
+                        rhs=moving(2, a), rhs_scale=picked_sc[2][4 * a :, whole],
                         start=a == 0, stop=a == 1,
                     )
             a_sb = keep.tile([P, COLS, 4], F32, name="a_sb", tag=f"a_sb{s}", align_bytes=64)
@@ -218,10 +224,10 @@ def tile_list_ligand_affinity_response_kernel(
             nc.scalar.activation(square[:], diff[:], ACT.Square)
             affinity = keep.tile([P, COLS, 4], F32, name="affinity", tag=f"affinity{s}", align_bytes=64)
             nc.scalar.activation(affinity[:], square[:], ACT.Exp, scale=-1.0)
-            h_bf = keep.tile([P, COLS, 4], BF16, name="h_bf", tag=f"diff{s + 1}" if s < HELD else f"h_bf{s}", align_bytes=64)
+            h_bf = keep.tile([P, COLS, 4], BF16, name="h_bf", tag=f"h_bf{s}", align_bytes=64)
             nc.vector.tensor_tensor(h_bf[:], affinity[:], c_ps[:].rearrange("p t j -> p j t"), ALU.mult)
-            h_codes = work.tile([P, COLS], U32, name="h_codes", align_bytes=64, bufs=3)
-            h_sc = work.tile([P, COLS], U8, name="h_sc", align_bytes=64, bufs=3)
+            h_codes = hstage.tile([P, COLS], U32, name="h_codes", align_bytes=64)
+            h_sc = hstage.tile([P, COLS], U8, name="h_sc", align_bytes=64)
             nc.vector.quantize_mx(h_codes[:].bitcast(FP8X4), h_sc[:], h_bf[:].rearrange("p j t -> p (j t)"))
             return h_codes, h_sc
 
@@ -229,7 +235,7 @@ def tile_list_ligand_affinity_response_kernel(
             whole = slice(s * COLS, (s + 1) * COLS)
             y_codes = ystage.tile([P, 2, COLS], U32, name="y_codes", align_bytes=64)
             for g in range(2):
-                y_ps = psum.tile([P, 4, COLS], F32, name="y_ps", bufs=PB[3])
+                y_ps = psum.tile([P, 4, COLS], F32, name="y_ps")
                 for u in range(4):
                     rows = slice(P * u, P * (u + 1))
                     nc.tensor.matmul_mx(
@@ -242,24 +248,27 @@ def tile_list_ligand_affinity_response_kernel(
                 nc.scalar.copy(y_sb[:], y_ps[:])
                 nc.sync.dma_start(y_rows[g][:, :, whole], y_sb[:])
                 y_bf = ystage.tile([P, COLS, 4], BF16, name="y_bf", align_bytes=64)
-                engine = YCAST(s, g)
-                source = y_ps if engine == "scalar" else y_sb
-                round_copy(nc, engine, y_bf[:], source[:].rearrange("p u j -> p j u"))
+                if 2 * s + g < ROUNDED_ON_SCALAR:
+                    nc.scalar.copy(y_bf[:], y_ps[:].rearrange("p u j -> p j u"))
+                else:
+                    nc.vector.tensor_copy(
+                        y_bf[:].rearrange("p (c i) u -> p c u i", i=4), y_sb[:].rearrange("p u (c i) -> p c u i", i=4)
+                    )
                 nc.vector.quantize_mx(
                     y_codes[:, g, :].bitcast(FP8X4), y_sc[:, g, whole], y_bf[:].rearrange("p j u -> p (j u)")
                 )
             nc.sync.dma_start(y_words[:, :, whole], y_codes[:].bitcast(I32))
 
-        steps = S // COLS
-        for s in range(steps):
-            h_codes, h_sc = first_stage(s)
-            for (step, kind), (c, x, a) in zip(slots, late):
-                if step == s:
-                    gather(c, x, a, f"{kind}{s}")
-            if s == 0:
-                prepare_wd(0)
-                prepare_wd(1)
-            second_stage(s, h_codes, h_sc)
+        quantised_h = []
+        for s in range(STEPS + LAG):
+            if s < STEPS:
+                quantised_h.append(first_stage(s))
+                for donor, (c, x) in zip(DONORS, late[len(DONORS) * s :]):
+                    gather_second(c, x, f"{donor}{s}")
+            if s == 1:
+                quantise_wd(1, "second_words0")
+            if s >= LAG:
+                second_stage(s - LAG, *quantised_h[s - LAG])
 
         for q in range(4):
             engine = nc.sync if q % 2 == 0 else nc.scalar

@@ -20,9 +20,9 @@ P = 128
 PICK = 256
 COLS = 128
 STEPS = S // COLS
-LAG = 2
-ROUNDED_ON_SCALAR = 2
-DONORS = ("a_sb", "diff")
+LAG = 1
+ROUNDED_ON_SCALAR = 0
+DONORS = ("a_sb",)
 
 
 def tile_list_ligand_affinity_response_kernel(
@@ -47,17 +47,12 @@ def tile_list_ligand_affinity_response_kernel(
         w3_sc_raw = keep.tile([P, H], U8, name="w3_sc_raw")
         nb_sc_pass1 = keep.tile([P, S], U8, name="nb_sc_pass1", align_bytes=64)
         nc.vector.memset(tab_sc[:].bitcast(I32), 0)
-        nc.vector.memset(w2_sc_raw[:].bitcast(I32), 0)
         nc.vector.memset(nb_sc_pass1[:].bitcast(I32), 0)
+        nc.vector.memset(w2_sc_raw[:].bitcast(I32), 0)
         nc.vector.memset(w3_sc_raw[:].bitcast(I32), 0)
         for q in range(4):
             nc.scalar.dma_start(
                 tab_sc[32 * q : 32 * q + 8, :].bitcast(I32), tab_scales[:, 4 * q : 4 * q + 4, :].bitcast(I32)
-            )
-        for q in range(4):
-            nc.scalar.dma_start(
-                w2_sc_raw[32 * q : 32 * q + 4, :].bitcast(I32).rearrange("r (a e) -> r a e", a=2),
-                w2_scales[:, 4 * q : 4 * q + 4, :].bitcast(I32).rearrange("a r e -> r a e"),
             )
 
         tab = [keep.tile([P, T], U32, name=f"tab{a}", align_bytes=64) for a in range(2)]
@@ -98,8 +93,13 @@ def tile_list_ligand_affinity_response_kernel(
 
         load_w23()
         load_wd(0)
-        load_wd(1)
+        for q in range(4):
+            nc.sync.dma_start(
+                w2_sc_raw[32 * q : 32 * q + 4, :].bitcast(I32).rearrange("r (a e) -> r a e", a=2),
+                w2_scales[:, 4 * q : 4 * q + 4, :].bitcast(I32).rearrange("a r e -> r a e"),
+            )
         load_tab(1)
+        load_wd(1)
         for q in range(4):
             nc.sync.dma_start(
                 w3_sc_raw[32 * q : 32 * q + 8, :].bitcast(I32), w3_scales[:, 4 * q : 4 * q + 4, :].bitcast(I32)
@@ -170,9 +170,10 @@ def tile_list_ligand_affinity_response_kernel(
             nc.vector.tensor_copy(buf[:], tab[1][:].indirect(lists[x][:, c * PICK // 16 : (c + 1) * PICK // 16]))
             second_words[c, x] = buf
 
-        for x in range(3):
-            gather_second(0, x, f"second_words{x}")
-        late = [(c, x) for c in range(1, S // PICK) for x in range(3)]
+        for c in range(2):
+            for x in range(3):
+                gather_second(c, x, f"second_words{3 * c + x}")
+        late = [(c, x) for c in range(2, S // PICK) for x in range(3)]
 
         y_sc = keep.tile([P, 2, S], U8, name="y_sc", align_bytes=64)
         y_rows = out_0.rearrange("(g p u) j -> g p u j", g=2, u=4)
@@ -216,16 +217,21 @@ def tile_list_ligand_affinity_response_kernel(
                         rhs=moving(2, a), rhs_scale=picked_sc[2][4 * a :, whole],
                         start=a == 0, stop=a == 1,
                     )
-            a_sb = keep.tile([P, COLS, 4], F32, name="a_sb", tag=f"a_sb{s}", align_bytes=64)
-            nc.scalar.copy(a_sb[:], a_ps[:].rearrange("p t j -> p j t"))
-            diff = keep.tile([P, COLS, 4], F32, name="diff", tag=f"diff{s}", align_bytes=64)
-            nc.vector.tensor_tensor(diff[:], a_sb[:], b_ps[:].rearrange("p t j -> p j t"), ALU.subtract)
-            square = keep.tile([P, COLS, 4], F32, name="square", tag=f"square{s}", align_bytes=64)
+            a_sb = keep.tile([P, 4, COLS], F32, name="a_sb", tag=f"a_sb{s}", align_bytes=64)
+            nc.scalar.copy(a_sb[:], a_ps[:])
+            diff = keep.tile([P, 4, COLS], F32, name="diff", tag=f"diff{s}", align_bytes=64)
+            nc.vector.tensor_tensor(diff[:], a_sb[:], b_ps[:], ALU.subtract)
+            square = keep.tile([P, 4, COLS], F32, name="square", tag=f"square{s}", align_bytes=64)
             nc.scalar.activation(square[:], diff[:], ACT.Square)
-            affinity = keep.tile([P, COLS, 4], F32, name="affinity", tag=f"affinity{s}", align_bytes=64)
+            affinity = keep.tile([P, 4, COLS], F32, name="affinity", tag=f"affinity{s}", align_bytes=64)
             nc.scalar.activation(affinity[:], square[:], ACT.Exp, scale=-1.0)
             h_bf = keep.tile([P, COLS, 4], BF16, name="h_bf", tag=f"h_bf{s}", align_bytes=64)
-            nc.vector.tensor_tensor(h_bf[:], affinity[:], c_ps[:].rearrange("p t j -> p j t"), ALU.mult)
+            nc.vector.tensor_tensor(
+                h_bf[:].rearrange("p (c i) t -> p c t i", i=2),
+                affinity[:].rearrange("p t (c i) -> p c t i", i=2),
+                c_ps[:].rearrange("p t (c i) -> p c t i", i=2),
+                ALU.mult,
+            )
             h_codes = hstage.tile([P, COLS], U32, name="h_codes", align_bytes=64)
             h_sc = hstage.tile([P, COLS], U8, name="h_sc", align_bytes=64)
             nc.vector.quantize_mx(h_codes[:].bitcast(FP8X4), h_sc[:], h_bf[:].rearrange("p j t -> p (j t)"))
@@ -249,7 +255,9 @@ def tile_list_ligand_affinity_response_kernel(
                 nc.sync.dma_start(y_rows[g][:, :, whole], y_sb[:])
                 y_bf = ystage.tile([P, COLS, 4], BF16, name="y_bf", align_bytes=64)
                 if 2 * s + g < ROUNDED_ON_SCALAR:
-                    nc.scalar.copy(y_bf[:], y_ps[:].rearrange("p u j -> p j u"))
+                    nc.scalar.copy(
+                        y_bf[:].rearrange("p (c i) u -> p c u i", i=2), y_ps[:].rearrange("p u (c i) -> p c u i", i=2)
+                    )
                 else:
                     nc.vector.tensor_copy(
                         y_bf[:].rearrange("p (c i) u -> p c u i", i=4), y_sb[:].rearrange("p u (c i) -> p c u i", i=4)

@@ -17,12 +17,16 @@ ACT = mybir.ActivationFunctionType
 ALU = mybir.AluOpType
 
 P = 128
-PICK = 256
+PASS = 512
 COLS = 128
 STEPS = S // COLS
-LAG = 1
-ROUNDED_ON_SCALAR = 0
-DONORS = ("a_sb",)
+PICK = 256
+FREE_CHUNKS = 2
+WD_ROUND = 32
+H_BUFS = 3
+Y_BUFS = 6
+PSUM_BUFS = 2
+CELL, NEIGHBOUR, LIGAND = 0, 1, 2
 
 
 def tile_list_ligand_affinity_response_kernel(
@@ -32,90 +36,81 @@ def tile_list_ligand_affinity_response_kernel(
     nc = tc.nc
     with ExitStack() as ctx:
         keep = ctx.enter_context(tc.tile_pool(name="keep", bufs=1))
-        hstage = ctx.enter_context(tc.tile_pool(name="hstage", bufs=3))
-        ystage = ctx.enter_context(tc.tile_pool(name="ystage", bufs=6))
-        psum = ctx.enter_context(tc.psum_pool(name="psum", bufs=2))
+        hstage = ctx.enter_context(tc.tile_pool(name="hstage", bufs=H_BUFS))
+        ystage = ctx.enter_context(tc.tile_pool(name="ystage", bufs=Y_BUFS))
+        psum = ctx.enter_context(tc.psum_pool(name="psum", bufs=PSUM_BUFS))
 
         lists = []
         for name, src in (("list1", offs), ("list2", offs2), ("list3", offs3)):
-            buf = keep.tile([P, S // 16], U16, name=name)
-            nc.sync.dma_start(buf[:], src)
-            lists.append(buf)
+            offsets = keep.tile([P, S // 16], U16, name=name)
+            nc.sync.dma_start(offsets[:], src)
+            lists.append(offsets)
 
         tab_sc = keep.tile([P, T], U8, name="tab_sc", align_bytes=64)
         w2_sc_raw = keep.tile([P, 2 * H], U8, name="w2_sc_raw")
         w3_sc_raw = keep.tile([P, H], U8, name="w3_sc_raw")
-        nb_sc_pass1 = keep.tile([P, S], U8, name="nb_sc_pass1", align_bytes=64)
+        neighbour_sc_pass1 = keep.tile([P, S], U8, name="neighbour_sc_pass1", align_bytes=64)
         nc.vector.memset(tab_sc[:].bitcast(I32), 0)
-        nc.vector.memset(nb_sc_pass1[:].bitcast(I32), 0)
-        nc.vector.memset(w2_sc_raw[:].bitcast(I32), 0)
-        nc.vector.memset(w3_sc_raw[:].bitcast(I32), 0)
+        nc.vector.memset(neighbour_sc_pass1[:].bitcast(I32), 0)
+        nc.gpsimd.memset(w2_sc_raw[:].bitcast(I32), 0)
+        nc.gpsimd.memset(w3_sc_raw[:].bitcast(I32), 0)
         for q in range(4):
-            nc.scalar.dma_start(
+            nc.sync.dma_start(
                 tab_sc[32 * q : 32 * q + 8, :].bitcast(I32), tab_scales[:, 4 * q : 4 * q + 4, :].bitcast(I32)
+            )
+        for q in range(4):
+            nc.sync.dma_start(
+                w2_sc_raw[32 * q : 32 * q + 4, :].bitcast(I32).rearrange("row (a w) -> row a w", a=2),
+                w2_scales[:, 4 * q : 4 * q + 4, :].bitcast(I32).rearrange("a row w -> row a w"),
+            )
+        for q in range(4):
+            nc.sync.dma_start(
+                w3_sc_raw[32 * q : 32 * q + 8, :].bitcast(I32), w3_scales[:, 4 * q : 4 * q + 4, :].bitcast(I32)
             )
 
         tab = [keep.tile([P, T], U32, name=f"tab{a}", align_bytes=64) for a in range(2)]
         w1_raw = [keep.tile([P, 4, H], F32, name=f"w1_raw{a}") for a in range(2)]
         w2_raw = keep.tile([P, 2, H // 2], I32, name="w2_raw")
         w3_raw = keep.tile([P, 2, H], I32, name="w3_raw")
-        wd_raw = [keep.tile([P, 4, 512], F32, name=f"wd_raw{g}") for g in range(2)]
+        wd_raw = [keep.tile([P, 4, PASS], F32, name=f"wd_raw{g}") for g in range(2)]
         wd_rows = wd.rearrange("(b t i) n -> t b i n", t=4, i=8)
+
+        def load_tab(a):
+            nc.sync.dma_start(tab[a][:].bitcast(I32), tab_words[a].rearrange("p col j -> p (col j)").bitcast(I32))
 
         def load_wd(g):
             for t in range(4):
-                nc.sync.dma_start(wd_raw[g][:, t, :], wd_rows[t][:, :, 512 * g : 512 * (g + 1)])
-
-        def load_tab(a):
-            nc.sync.dma_start(tab[a][:].bitcast(I32), tab_words[a].rearrange("p t i -> p (t i)").bitcast(I32))
-
-        def load_w1(a):
-            nc.sync.dma_start(w1_raw[a][:], w1[512 * a : 512 * (a + 1), :].rearrange("(p j) c -> p j c", j=4))
-
-        def load_w23():
-            nc.sync.dma_start(w2_raw[:], w2_words.bitcast(I32).rearrange("a p e -> p a e"))
-            nc.sync.dma_start(w3_raw[:], w3_words.rearrange("a p e i -> p a (e i)").bitcast(I32))
+                nc.sync.dma_start(wd_raw[g][:, t, :], wd_rows[t][:, :, PASS * g : PASS * (g + 1)])
 
         load_tab(0)
-        load_w1(0)
-        load_w1(1)
+        for a in range(2):
+            nc.sync.dma_start(w1_raw[a][:], w1[PASS * a : PASS * (a + 1), :].rearrange("(p j) r -> p j r", j=4))
 
-        picked_sc = [None, None, None]
-        for x in (1, 0, 2):
-            buf = keep.tile([P, S], U8, name=f"picked_sc{x}", align_bytes=64)
-            nc.vector.tensor_copy(buf[:], tab_sc[:].indirect(lists[x][:]))
-            picked_sc[x] = buf
+        picked_sc = {}
+        for x in (NEIGHBOUR, CELL, LIGAND):
+            picked_sc[x] = keep.tile([P, S], U8, name=f"picked_sc{x}", align_bytes=64)
+            nc.vector.tensor_copy(picked_sc[x][:], tab_sc[:].indirect(lists[x][:]))
         for q in range(4):
             nc.sync.dma_start(
-                nb_sc_pass1[32 * q : 32 * q + 4, :].bitcast(I32),
-                picked_sc[1][32 * q + 4 : 32 * q + 8, :].bitcast(I32),
+                neighbour_sc_pass1[32 * q : 32 * q + 4, :].bitcast(I32),
+                picked_sc[NEIGHBOUR][32 * q + 4 : 32 * q + 8, :].bitcast(I32),
             )
 
-        load_w23()
+        nc.sync.dma_start(w2_raw[:], w2_words.bitcast(I32).rearrange("a p w -> p a w"))
+        nc.sync.dma_start(w3_raw[:], w3_words.rearrange("a p r j -> p a (r j)").bitcast(I32))
         load_wd(0)
-        for q in range(4):
-            nc.sync.dma_start(
-                w2_sc_raw[32 * q : 32 * q + 4, :].bitcast(I32).rearrange("r (a e) -> r a e", a=2),
-                w2_scales[:, 4 * q : 4 * q + 4, :].bitcast(I32).rearrange("a r e -> r a e"),
-            )
         load_tab(1)
         load_wd(1)
-        for q in range(4):
-            nc.sync.dma_start(
-                w3_sc_raw[32 * q : 32 * q + 8, :].bitcast(I32), w3_scales[:, 4 * q : 4 * q + 4, :].bitcast(I32)
-            )
 
         w1_codes, w1_sc = [], []
         for a in range(2):
-            grouped = keep.tile([P, 4, 4 * P], BF16, name=f"w1_bf{a}", align_bytes=64)
-            source = w1_raw[a][:].rearrange("p j (b t h i) -> p t b h j i", t=4, h=2, i=4)
+            w1_bf = keep.tile([P, 4, 4 * P], BF16, name=f"w1_bf{a}", align_bytes=64)
+            source = w1_raw[a][:].rearrange("p j (b t f e) -> p t b f j e", t=4, f=2, e=4)
             for t in range(4):
-                nc.scalar.copy(grouped[:, t, :].rearrange("p (b h i j) -> p b h j i", h=2, i=4, j=4), source[:, t])
-            codes = keep.tile([P, H], U32, name=f"w1_codes{a}", align_bytes=64)
-            sc = keep.tile([P, H], U8, name=f"w1_sc{a}", align_bytes=64)
-            nc.vector.quantize_mx(codes[:].bitcast(FP8X4), sc[:], grouped[:].rearrange("p t e -> p (t e)"))
-            w1_codes.append(codes)
-            w1_sc.append(sc)
+                nc.scalar.copy(w1_bf[:, t, :].rearrange("p (b f e j) -> p b f j e", f=2, e=4, j=4), source[:, t])
+            w1_codes.append(keep.tile([P, H], U32, name=f"w1_codes{a}", align_bytes=64))
+            w1_sc.append(keep.tile([P, H], U8, name=f"w1_sc{a}", align_bytes=64))
+            nc.vector.quantize_mx(w1_codes[a][:].bitcast(FP8X4), w1_sc[a][:], w1_bf[:].rearrange("p t v -> p (t v)"))
 
         w2_codes = keep.tile([P, 2, 2 * H], U8, name="w2_codes", align_bytes=64)
         w3_codes = keep.tile([P, 2, H], U32, name="w3_codes", align_bytes=64)
@@ -141,50 +136,46 @@ def tile_list_ligand_affinity_response_kernel(
 
         first_words = []
         for x in range(3):
-            buf = keep.tile([P, S], U32, name=f"first_words{x}", align_bytes=64)
-            nc.vector.tensor_copy(buf[:], tab[0][:].indirect(lists[x][:]))
-            first_words.append(buf)
+            first_words.append(keep.tile([P, S], U32, name=f"first_words{x}", align_bytes=64))
+            nc.vector.tensor_copy(first_words[x][:], tab[0][:].indirect(lists[x][:]))
 
         wd_bf, wd_codes, wd_sc = [], [], []
         for g in range(2):
-            grouped = keep.tile([P, 4 * 512], BF16, name=f"wd_bf{g}", align_bytes=64)
-            dst = grouped[:].rearrange("p (u m t) -> p m t u", u=4, t=4)
-            src = wd_raw[g][:].rearrange("p t (m u) -> p m t u", u=4)
-            for m0 in range(0, P, 32):
-                nc.scalar.copy(dst[:, m0 : m0 + 32], src[:, m0 : m0 + 32])
-            wd_bf.append(grouped)
+            wd_bf.append(keep.tile([P, 4 * PASS], BF16, name=f"wd_bf{g}", align_bytes=64))
+            dealt = wd_bf[g][:].rearrange("p (u m t) -> p m t u", u=4, t=4)
+            loaded = wd_raw[g][:].rearrange("p t (m u) -> p m t u", u=4)
+            for m0 in range(0, P, WD_ROUND):
+                nc.scalar.copy(dealt[:, m0 : m0 + WD_ROUND], loaded[:, m0 : m0 + WD_ROUND])
 
         def quantise_wd(g, tag):
-            codes = keep.tile([P, 512], U32, name=f"wd_codes{g}", tag=tag, align_bytes=64)
-            sc = keep.tile([P, 512], U8, name=f"wd_sc{g}", align_bytes=64)
-            nc.vector.quantize_mx(codes[:].bitcast(FP8X4), sc[:], wd_bf[g][:])
-            wd_codes.append(codes)
-            wd_sc.append(sc)
+            wd_codes.append(keep.tile([P, PASS], U32, name=f"wd_codes{g}", tag=tag, align_bytes=64))
+            wd_sc.append(keep.tile([P, PASS], U8, name=f"wd_sc{g}", align_bytes=64))
+            nc.vector.quantize_mx(wd_codes[g][:].bitcast(FP8X4), wd_sc[g][:], wd_bf[g][:])
 
         quantise_wd(0, "wd_codes0")
 
         second_words = {}
 
-        def gather_second(c, x, tag):
-            buf = keep.tile([P, PICK], U32, name=f"second_words{c}{x}", tag=tag, align_bytes=64)
-            nc.vector.tensor_copy(buf[:], tab[1][:].indirect(lists[x][:, c * PICK // 16 : (c + 1) * PICK // 16]))
-            second_words[c, x] = buf
+        def gather_second(chunk, x, tag):
+            entries = slice(chunk * PICK // 16, (chunk + 1) * PICK // 16)
+            second_words[chunk, x] = keep.tile([P, PICK], U32, name=f"second_words{chunk}{x}", tag=tag, align_bytes=64)
+            nc.vector.tensor_copy(second_words[chunk, x][:], tab[1][:].indirect(lists[x][:, entries]))
 
-        for c in range(2):
+        for chunk in range(FREE_CHUNKS):
             for x in range(3):
-                gather_second(c, x, f"second_words{3 * c + x}")
-        late = [(c, x) for c in range(2, S // PICK) for x in range(3)]
+                gather_second(chunk, x, f"second_words{chunk}{x}")
+        held = [(chunk, x) for chunk in range(FREE_CHUNKS, S // PICK) for x in range(3)]
 
         y_sc = keep.tile([P, 2, S], U8, name="y_sc", align_bytes=64)
-        y_rows = out_0.rearrange("(g p u) j -> g p u j", g=2, u=4)
-        y_words = out_1.rearrange("g p m t -> p g (m t)").bitcast(I32)
+        y_rows = out_0.rearrange("(g m u) col -> g m u col", g=2, u=4)
+        y_words = out_1.rearrange("g m col u -> m g (col u)").bitcast(I32)
 
         def first_stage(s):
-            whole = slice(s * COLS, (s + 1) * COLS)
-            within = slice(s * COLS % PICK, s * COLS % PICK + COLS)
+            cols = slice(s * COLS, (s + 1) * COLS)
+            cols_in_chunk = slice(s * COLS % PICK, s * COLS % PICK + COLS)
 
             def moving(x, a):
-                words = first_words[x][:, whole] if a == 0 else second_words[s * COLS // PICK, x][:, within]
+                words = first_words[x][:, cols] if a == 0 else second_words[s * COLS // PICK, x][:, cols_in_chunk]
                 return words.bitcast(FP8X4)
 
             a_ps = psum.tile([P, 4, COLS], F32, name="a_ps")
@@ -196,16 +187,17 @@ def tile_list_ligand_affinity_response_kernel(
                     nc.tensor.matmul_mx(
                         a_ps[:, t, :],
                         lhsT=w1_codes[a][:, rows].bitcast(FP8X4), lhsT_scale=w1_sc[a][:, rows],
-                        rhs=moving(0, a), rhs_scale=picked_sc[0][4 * a :, whole],
+                        rhs=moving(CELL, a), rhs_scale=picked_sc[CELL][4 * a :, cols],
                         start=a == 0, stop=a == 1,
                     )
             for t in range(4):
                 rows = slice(P * t, P * (t + 1))
+                row_bytes = slice(2 * P * t, 2 * P * (t + 1))
                 for a in range(2):
                     nc.tensor.matmul_mx(
                         b_ps[:, t, :],
-                        lhsT=w2_codes[:, a, 2 * P * t : 2 * P * (t + 1)].bitcast(FP4X4), lhsT_scale=w2_sc[:, a, rows],
-                        rhs=moving(1, a), rhs_scale=(picked_sc[1], nb_sc_pass1)[a][:, whole],
+                        lhsT=w2_codes[:, a, row_bytes].bitcast(FP4X4), lhsT_scale=w2_sc[:, a, rows],
+                        rhs=moving(NEIGHBOUR, a), rhs_scale=(picked_sc[NEIGHBOUR], neighbour_sc_pass1)[a][:, cols],
                         start=a == 0, stop=a == 1,
                     )
             for t in range(4):
@@ -214,9 +206,10 @@ def tile_list_ligand_affinity_response_kernel(
                     nc.tensor.matmul_mx(
                         c_ps[:, t, :],
                         lhsT=w3_codes[:, a, rows].bitcast(FP8X4), lhsT_scale=w3_sc[4 * a :, rows],
-                        rhs=moving(2, a), rhs_scale=picked_sc[2][4 * a :, whole],
+                        rhs=moving(LIGAND, a), rhs_scale=picked_sc[LIGAND][4 * a :, cols],
                         start=a == 0, stop=a == 1,
                     )
+
             a_sb = keep.tile([P, 4, COLS], F32, name="a_sb", tag=f"a_sb{s}", align_bytes=64)
             nc.scalar.copy(a_sb[:], a_ps[:])
             diff = keep.tile([P, 4, COLS], F32, name="diff", tag=f"diff{s}", align_bytes=64)
@@ -225,20 +218,21 @@ def tile_list_ligand_affinity_response_kernel(
             nc.scalar.activation(square[:], diff[:], ACT.Square)
             affinity = keep.tile([P, 4, COLS], F32, name="affinity", tag=f"affinity{s}", align_bytes=64)
             nc.scalar.activation(affinity[:], square[:], ACT.Exp, scale=-1.0)
+
             h_bf = keep.tile([P, COLS, 4], BF16, name="h_bf", tag=f"h_bf{s}", align_bytes=64)
             nc.vector.tensor_tensor(
-                h_bf[:].rearrange("p (c i) t -> p c t i", i=2),
-                affinity[:].rearrange("p t (c i) -> p c t i", i=2),
-                c_ps[:].rearrange("p t (c i) -> p c t i", i=2),
+                h_bf[:].rearrange("p (pair e) t -> p pair t e", e=2),
+                affinity[:].rearrange("p t (pair e) -> p pair t e", e=2),
+                c_ps[:].rearrange("p t (pair e) -> p pair t e", e=2),
                 ALU.mult,
             )
             h_codes = hstage.tile([P, COLS], U32, name="h_codes", align_bytes=64)
             h_sc = hstage.tile([P, COLS], U8, name="h_sc", align_bytes=64)
-            nc.vector.quantize_mx(h_codes[:].bitcast(FP8X4), h_sc[:], h_bf[:].rearrange("p j t -> p (j t)"))
+            nc.vector.quantize_mx(h_codes[:].bitcast(FP8X4), h_sc[:], h_bf[:].rearrange("p col t -> p (col t)"))
             return h_codes, h_sc
 
         def second_stage(s, h_codes, h_sc):
-            whole = slice(s * COLS, (s + 1) * COLS)
+            cols = slice(s * COLS, (s + 1) * COLS)
             y_codes = ystage.tile([P, 2, COLS], U32, name="y_codes", align_bytes=64)
             for g in range(2):
                 y_ps = psum.tile([P, 4, COLS], F32, name="y_ps")
@@ -252,35 +246,31 @@ def tile_list_ligand_affinity_response_kernel(
                     )
                 y_sb = ystage.tile([P, 4, COLS], F32, name="y_sb")
                 nc.scalar.copy(y_sb[:], y_ps[:])
-                nc.sync.dma_start(y_rows[g][:, :, whole], y_sb[:])
+                nc.sync.dma_start(y_rows[g][:, :, cols], y_sb[:])
                 y_bf = ystage.tile([P, COLS, 4], BF16, name="y_bf", align_bytes=64)
-                if 2 * s + g < ROUNDED_ON_SCALAR:
-                    nc.scalar.copy(
-                        y_bf[:].rearrange("p (c i) u -> p c u i", i=2), y_ps[:].rearrange("p u (c i) -> p c u i", i=2)
-                    )
-                else:
-                    nc.vector.tensor_copy(
-                        y_bf[:].rearrange("p (c i) u -> p c u i", i=4), y_sb[:].rearrange("p u (c i) -> p c u i", i=4)
-                    )
-                nc.vector.quantize_mx(
-                    y_codes[:, g, :].bitcast(FP8X4), y_sc[:, g, whole], y_bf[:].rearrange("p j u -> p (j u)")
+                nc.vector.tensor_copy(
+                    y_bf[:].rearrange("p (four e) u -> p four u e", e=4),
+                    y_sb[:].rearrange("p u (four e) -> p four u e", e=4),
                 )
-            nc.sync.dma_start(y_words[:, :, whole], y_codes[:].bitcast(I32))
+                nc.vector.quantize_mx(
+                    y_codes[:, g, :].bitcast(FP8X4), y_sc[:, g, cols], y_bf[:].rearrange("p col u -> p (col u)")
+                )
+            nc.sync.dma_start(y_words[:, :, cols], y_codes[:].bitcast(I32))
 
         quantised_h = []
-        for s in range(STEPS + LAG):
+        for s in range(STEPS + 1):
             if s < STEPS:
                 quantised_h.append(first_stage(s))
-                for donor, (c, x) in zip(DONORS, late[len(DONORS) * s :]):
-                    gather_second(c, x, f"{donor}{s}")
-            if s == 1:
-                quantise_wd(1, "second_words0")
-            if s >= LAG:
-                second_stage(s - LAG, *quantised_h[s - LAG])
+            if s < len(held):
+                gather_second(*held[s], f"diff{s}")
+            if s == PICK // COLS - 1:
+                quantise_wd(1, f"second_words0{CELL}")
+            if s >= 1:
+                second_stage(s - 1, *quantised_h[s - 1])
 
         for q in range(4):
-            engine = nc.sync if q % 2 == 0 else nc.scalar
-            engine.dma_start(
-                out_2[:, 4 * q : 4 * q + 4, :].bitcast(I32).rearrange("g r m -> r g m"),
+            queue = nc.sync if q % 2 == 0 else nc.scalar
+            queue.dma_start(
+                out_2[:, 4 * q : 4 * q + 4, :].bitcast(I32).rearrange("g row col -> row g col"),
                 y_sc[32 * q : 32 * q + 4, :, :].bitcast(I32),
             )

from contextlib import ExitStack

import concourse.mybir as mybir

K, H, N, T, S = 1024, 512, 1024, 2048, 1024
FLOPS = 2 * S * (3 * K * H + H * N)

F32 = mybir.dt.float32
BF16 = mybir.dt.bfloat16
I32 = mybir.dt.int32
U32 = mybir.dt.uint32
U16 = mybir.dt.uint16
U8 = mybir.dt.uint8
FP8X4 = mybir.dt.float8_e4m3fn_x4
FP4X4 = mybir.dt.float4_e2m1fn_x4
ACT = mybir.ActivationFunctionType
ALU = mybir.AluOpType

P = 128
PASS = 512
COLS = 128
STEPS = S // COLS
PICK = 256
FREE_CHUNKS = 2
WD_ROUND = 32
H_BUFS = 3
Y_BUFS = 6
PSUM_BUFS = 2
CELL, NEIGHBOUR, LIGAND = 0, 1, 2


def tile_list_ligand_affinity_response_kernel(
    tc, tab_words, tab_scales, offs, offs2, offs3, w1, w2_words, w2_scales, w3_words, w3_scales, wd,
    out_0, out_1, out_2,
):
    nc = tc.nc
    with ExitStack() as ctx:
        keep = ctx.enter_context(tc.tile_pool(name="keep", bufs=1))
        hstage = ctx.enter_context(tc.tile_pool(name="hstage", bufs=H_BUFS))
        ystage = ctx.enter_context(tc.tile_pool(name="ystage", bufs=Y_BUFS))
        psum = ctx.enter_context(tc.psum_pool(name="psum", bufs=PSUM_BUFS))

        lists = []
        for name, src in (("list1", offs), ("list2", offs2), ("list3", offs3)):
            offsets = keep.tile([P, S // 16], U16, name=name)
            nc.sync.dma_start(offsets[:], src)
            lists.append(offsets)

        tab_sc = keep.tile([P, T], U8, name="tab_sc", align_bytes=64)
        w2_sc_raw = keep.tile([P, 2 * H], U8, name="w2_sc_raw")
        w3_sc_raw = keep.tile([P, H], U8, name="w3_sc_raw")
        neighbour_sc_pass1 = keep.tile([P, S], U8, name="neighbour_sc_pass1", align_bytes=64)
        nc.vector.memset(tab_sc[:].bitcast(I32), 0)
        nc.vector.memset(neighbour_sc_pass1[:].bitcast(I32), 0)
        nc.gpsimd.memset(w2_sc_raw[:].bitcast(I32), 0)
        nc.gpsimd.memset(w3_sc_raw[:].bitcast(I32), 0)
        for q in range(4):
            nc.sync.dma_start(
                tab_sc[32 * q : 32 * q + 8, :].bitcast(I32), tab_scales[:, 4 * q : 4 * q + 4, :].bitcast(I32)
            )
        for q in range(4):
            nc.sync.dma_start(
                w2_sc_raw[32 * q : 32 * q + 4, :].bitcast(I32).rearrange("row (a w) -> row a w", a=2),
                w2_scales[:, 4 * q : 4 * q + 4, :].bitcast(I32).rearrange("a row w -> row a w"),
            )
        for q in range(4):
            nc.sync.dma_start(
                w3_sc_raw[32 * q : 32 * q + 8, :].bitcast(I32), w3_scales[:, 4 * q : 4 * q + 4, :].bitcast(I32)
            )

        tab = [keep.tile([P, T], U32, name=f"tab{a}", align_bytes=64) for a in range(2)]
        w1_raw = [keep.tile([P, 4, H], F32, name=f"w1_raw{a}") for a in range(2)]
        w2_raw = keep.tile([P, 2, H // 2], I32, name="w2_raw")
        w3_raw = keep.tile([P, 2, H], I32, name="w3_raw")
        wd_raw = [keep.tile([P, 4, PASS], F32, name=f"wd_raw{g}") for g in range(2)]
        wd_rows = wd.rearrange("(b t i) n -> t b i n", t=4, i=8)

        def load_tab(a):
            nc.sync.dma_start(tab[a][:].bitcast(I32), tab_words[a].rearrange("p col j -> p (col j)").bitcast(I32))

        def load_wd(g):
            for t in range(4):
                nc.sync.dma_start(wd_raw[g][:, t, :], wd_rows[t][:, :, PASS * g : PASS * (g + 1)])

        load_tab(0)
        for a in range(2):
            nc.sync.dma_start(w1_raw[a][:], w1[PASS * a : PASS * (a + 1), :].rearrange("(p j) r -> p j r", j=4))

        picked_sc = {}
        for x in (NEIGHBOUR, CELL, LIGAND):
            picked_sc[x] = keep.tile([P, S], U8, name=f"picked_sc{x}", align_bytes=64)
            nc.vector.tensor_copy(picked_sc[x][:], tab_sc[:].indirect(lists[x][:]))
        for q in range(4):
            nc.sync.dma_start(
                neighbour_sc_pass1[32 * q : 32 * q + 4, :].bitcast(I32),
                picked_sc[NEIGHBOUR][32 * q + 4 : 32 * q + 8, :].bitcast(I32),
            )

        nc.sync.dma_start(w2_raw[:], w2_words.bitcast(I32).rearrange("a p w -> p a w"))
        nc.sync.dma_start(w3_raw[:], w3_words.rearrange("a p r j -> p a (r j)").bitcast(I32))
        load_wd(0)
        load_tab(1)
        load_wd(1)

        w1_codes, w1_sc = [], []
        for a in range(2):
            w1_bf = keep.tile([P, 4, 4 * P], BF16, name=f"w1_bf{a}", align_bytes=64)
            source = w1_raw[a][:].rearrange("p j (b t f e) -> p t b f j e", t=4, f=2, e=4)
            for t in range(4):
                nc.scalar.copy(w1_bf[:, t, :].rearrange("p (b f e j) -> p b f j e", f=2, e=4, j=4), source[:, t])
            w1_codes.append(keep.tile([P, H], U32, name=f"w1_codes{a}", align_bytes=64))
            w1_sc.append(keep.tile([P, H], U8, name=f"w1_sc{a}", align_bytes=64))
            nc.vector.quantize_mx(w1_codes[a][:].bitcast(FP8X4), w1_sc[a][:], w1_bf[:].rearrange("p t v -> p (t v)"))

        w2_codes = keep.tile([P, 2, 2 * H], U8, name="w2_codes", align_bytes=64)
        w3_codes = keep.tile([P, 2, H], U32, name="w3_codes", align_bytes=64)
        w2_sc = keep.tile([P, 2, H], U8, name="w2_sc", align_bytes=64)
        w3_sc = keep.tile([P, H], U8, name="w3_sc", align_bytes=64)
        nc.scalar.copy(
            w2_codes[:].bitcast(U32).rearrange("p a (t b w) -> p a t b w", t=4, w=4),
            w2_raw[:].bitcast(U32).rearrange("p a (b t w) -> p a t b w", t=4, w=4),
        )
        for a in range(2):
            nc.scalar.copy(
                w3_codes[:, a, :].rearrange("p (t b w) -> p t b w", t=4, w=8),
                w3_raw[:, a, :].bitcast(U32).rearrange("p (b t w) -> p t b w", t=4, w=8),
            )
        nc.scalar.copy(
            w2_sc[:].bitcast(U32).rearrange("p a (t b w) -> p a t b w", t=4, w=2),
            w2_sc_raw[:].bitcast(U32).rearrange("p (a b t w) -> p a t b w", a=2, t=4, w=2),
        )
        nc.scalar.copy(
            w3_sc[:].bitcast(U32).rearrange("p (t b w) -> p t b w", t=4, w=2),
            w3_sc_raw[:].bitcast(U32).rearrange("p (b t w) -> p t b w", t=4, w=2),
        )

        first_words = []
        for x in range(3):
            first_words.append(keep.tile([P, S], U32, name=f"first_words{x}", align_bytes=64))
            nc.vector.tensor_copy(first_words[x][:], tab[0][:].indirect(lists[x][:]))

        wd_bf, wd_codes, wd_sc = [], [], []
        for g in range(2):
            wd_bf.append(keep.tile([P, 4 * PASS], BF16, name=f"wd_bf{g}", align_bytes=64))
            dealt = wd_bf[g][:].rearrange("p (u m t) -> p m t u", u=4, t=4)
            loaded = wd_raw[g][:].rearrange("p t (m u) -> p m t u", u=4)
            for m0 in range(0, P, WD_ROUND):
                nc.scalar.copy(dealt[:, m0 : m0 + WD_ROUND], loaded[:, m0 : m0 + WD_ROUND])

        def quantise_wd(g, tag):
            wd_codes.append(keep.tile([P, PASS], U32, name=f"wd_codes{g}", tag=tag, align_bytes=64))
            wd_sc.append(keep.tile([P, PASS], U8, name=f"wd_sc{g}", align_bytes=64))
            nc.vector.quantize_mx(wd_codes[g][:].bitcast(FP8X4), wd_sc[g][:], wd_bf[g][:])

        quantise_wd(0, "wd_codes0")

        second_words = {}

        def gather_second(chunk, x, tag):
            entries = slice(chunk * PICK // 16, (chunk + 1) * PICK // 16)
            second_words[chunk, x] = keep.tile([P, PICK], U32, name=f"second_words{chunk}{x}", tag=tag, align_bytes=64)
            nc.vector.tensor_copy(second_words[chunk, x][:], tab[1][:].indirect(lists[x][:, entries]))

        for chunk in range(FREE_CHUNKS):
            for x in range(3):
                gather_second(chunk, x, f"second_words{chunk}{x}")
        held = [(chunk, x) for chunk in range(FREE_CHUNKS, S // PICK) for x in range(3)]

        y_sc = keep.tile([P, 2, S], U8, name="y_sc", align_bytes=64)
        y_rows = out_0.rearrange("(g m u) col -> g m u col", g=2, u=4)
        y_words = out_1.rearrange("g m col u -> m g (col u)").bitcast(I32)

        def first_stage(s):
            cols = slice(s * COLS, (s + 1) * COLS)
            cols_in_chunk = slice(s * COLS % PICK, s * COLS % PICK + COLS)

            def moving(x, a):
                words = first_words[x][:, cols] if a == 0 else second_words[s * COLS // PICK, x][:, cols_in_chunk]
                return words.bitcast(FP8X4)

            a_ps = psum.tile([P, 4, COLS], F32, name="a_ps")
            b_ps = psum.tile([P, 4, COLS], F32, name="b_ps")
            c_ps = psum.tile([P, 4, COLS], F32, name="c_ps")
            for t in range(4):
                rows = slice(P * t, P * (t + 1))
                for a in range(2):
                    nc.tensor.matmul_mx(
                        a_ps[:, t, :],
                        lhsT=w1_codes[a][:, rows].bitcast(FP8X4), lhsT_scale=w1_sc[a][:, rows],
                        rhs=moving(CELL, a), rhs_scale=picked_sc[CELL][4 * a :, cols],
                        start=a == 0, stop=a == 1,
                    )
            for t in range(4):
                rows = slice(P * t, P * (t + 1))
                row_bytes = slice(2 * P * t, 2 * P * (t + 1))
                for a in range(2):
                    nc.tensor.matmul_mx(
                        b_ps[:, t, :],
                        lhsT=w2_codes[:, a, row_bytes].bitcast(FP4X4), lhsT_scale=w2_sc[:, a, rows],
                        rhs=moving(NEIGHBOUR, a), rhs_scale=(picked_sc[NEIGHBOUR], neighbour_sc_pass1)[a][:, cols],
                        start=a == 0, stop=a == 1,
                    )
            for t in range(4):
                rows = slice(P * t, P * (t + 1))
                for a in range(2):
                    nc.tensor.matmul_mx(
                        c_ps[:, t, :],
                        lhsT=w3_codes[:, a, rows].bitcast(FP8X4), lhsT_scale=w3_sc[4 * a :, rows],
                        rhs=moving(LIGAND, a), rhs_scale=picked_sc[LIGAND][4 * a :, cols],
                        start=a == 0, stop=a == 1,
                    )

            a_sb = keep.tile([P, 4, COLS], F32, name="a_sb", tag=f"a_sb{s}", align_bytes=64)
            nc.scalar.copy(a_sb[:], a_ps[:])
            diff = keep.tile([P, 4, COLS], F32, name="diff", tag=f"diff{s}", align_bytes=64)
            nc.vector.tensor_tensor(diff[:], a_sb[:], b_ps[:], ALU.subtract)
            square = keep.tile([P, 4, COLS], F32, name="square", tag=f"square{s}", align_bytes=64)
            nc.scalar.activation(square[:], diff[:], ACT.Square)
            affinity = keep.tile([P, 4, COLS], F32, name="affinity", tag=f"affinity{s}", align_bytes=64)
            nc.scalar.activation(affinity[:], square[:], ACT.Exp, scale=-1.0)

            h_bf = keep.tile([P, COLS, 4], BF16, name="h_bf", tag=f"h_bf{s}", align_bytes=64)
            nc.vector.tensor_tensor(
                h_bf[:].rearrange("p (pair e) t -> p pair t e", e=2),
                affinity[:].rearrange("p t (pair e) -> p pair t e", e=2),
                c_ps[:].rearrange("p t (pair e) -> p pair t e", e=2),
                ALU.mult,
            )
            h_codes = hstage.tile([P, COLS], U32, name="h_codes", align_bytes=64)
            h_sc = hstage.tile([P, COLS], U8, name="h_sc", align_bytes=64)
            nc.vector.quantize_mx(h_codes[:].bitcast(FP8X4), h_sc[:], h_bf[:].rearrange("p col t -> p (col t)"))
            return h_codes, h_sc

        def second_stage(s, h_codes, h_sc):
            cols = slice(s * COLS, (s + 1) * COLS)
            y_codes = ystage.tile([P, 2, COLS], U32, name="y_codes", align_bytes=64)
            for g in range(2):
                y_ps = psum.tile([P, 4, COLS], F32, name="y_ps")
                for u in range(4):
                    rows = slice(P * u, P * (u + 1))
                    nc.tensor.matmul_mx(
                        y_ps[:, u, :],
                        lhsT=wd_codes[g][:, rows].bitcast(FP8X4), lhsT_scale=wd_sc[g][:, rows],
                        rhs=h_codes[:].bitcast(FP8X4), rhs_scale=h_sc[:],
                        start=True, stop=True,
                    )
                y_sb = ystage.tile([P, 4, COLS], F32, name="y_sb")
                nc.scalar.copy(y_sb[:], y_ps[:])
                nc.sync.dma_start(y_rows[g][:, :, cols], y_sb[:])
                y_bf = ystage.tile([P, COLS, 4], BF16, name="y_bf", align_bytes=64)
                nc.vector.tensor_copy(
                    y_bf[:].rearrange("p (four e) u -> p four u e", e=4),
                    y_sb[:].rearrange("p u (four e) -> p four u e", e=4),
                )
                nc.vector.quantize_mx(
                    y_codes[:, g, :].bitcast(FP8X4), y_sc[:, g, cols], y_bf[:].rearrange("p col u -> p (col u)")
                )
            nc.sync.dma_start(y_words[:, :, cols], y_codes[:].bitcast(I32))

        quantised_h = []
        for s in range(STEPS + 1):
            if s < STEPS:
                quantised_h.append(first_stage(s))
            if s < len(held):
                gather_second(*held[s], f"diff{s}")
            if s == PICK // COLS - 1:
                quantise_wd(1, f"second_words0{CELL}")
            if s >= 1:
                second_stage(s - 1, *quantised_h[s - 1])

        for q in range(4):
            queue = nc.sync if q % 2 == 0 else nc.scalar
            queue.dma_start(
                out_2[:, 4 * q : 4 * q + 4, :].bitcast(I32).rearrange("g row col -> row g col"),
                y_sc[32 * q : 32 * q + 4, :, :].bitcast(I32),
            )
